import numpy as np
import ml_dtypes


def mxq(x, axis, fmt="e4m3"):
    dtype, down = {"e4m3": (ml_dtypes.float8_e4m3fn, 7), "e5m2": (ml_dtypes.float8_e5m2, 14)}[fmt]
    v = np.moveaxis(np.asarray(x, np.float32).astype(ml_dtypes.bfloat16).astype(np.float64), axis, -1)
    blocks = v.reshape(v.shape[:-1] + (-1, 32))
    amax = np.abs(blocks).max(-1, keepdims=True)
    byte = np.maximum(np.where(amax > 0, np.frexp(amax)[1] - 1 + 127, 0) - down, 1)
    scale = np.exp2(byte - 127.0)
    codes = (blocks / scale).astype(np.float32).astype(dtype).astype(np.float64)
    return np.moveaxis((codes * scale).reshape(v.shape), -1, axis)


WIDE = False


def mx_kscale(k):
    if not WIDE:
        return np.ones(k)
    levels = np.array([10, -10, 5, -5, 0])
    if k % 512:
        return np.exp2(np.random.permutation(np.resize(levels, k // 32))).repeat(32)
    a = np.empty((k // 512, 16))
    for p in range(k // 512):
        a[p, :8] = np.random.permutation(np.resize(levels, 8))
        for g in range(8):
            far = levels[np.abs(levels - a[p, g]) >= 10]
            a[p, g + 8] = far[np.random.randint(len(far))]
    return np.exp2(a.ravel()).repeat(32)


BF16 = ml_dtypes.bfloat16


def bf(x):
    return np.asarray(x, np.float32).astype(BF16)


def f64(x):
    return np.asarray(x).astype(np.float64)


B, D, H, C = 1024, 1024, 1024, 512


def draw0():
    s, t = mx_kscale(D), mx_kscale(H)
    return {
        "x": bf(np.random.standard_normal((B, D)) * s),
        "w1": bf(np.random.standard_normal((D, H)) * 1.2 / np.sqrt(D) / s[:, None]),
        "g1": bf((1.0 + 0.1 * np.random.standard_normal(H)) * t),
        "v1": bf(np.random.standard_normal((H, C)) / np.sqrt(H) / t[:, None]),
        "wx": bf(np.random.standard_normal((D, C)) * 0.8 / np.sqrt(D) / s[:, None]),
        "wh": bf(np.random.standard_normal((H, C)) * 1.2 / np.sqrt(H) / t[:, None]),
        "u": bf(np.random.standard_normal((B, C))),
    }


def centred_features(xq, w1, g1):
    r = np.maximum(xq @ mxq(f64(w1), 0, "e4m3"), 0.0)
    return (r - np.mean(r, axis=0, keepdims=True)) * f64(g1)[None, :]


def newton_target(y, score):
    return y * (1.0 + np.exp(-y * score))


def core(x, w1, g1, v1, wx, wh, u):
    xq = mxq(f64(x), 1, "e4m3")
    h = centred_features(xq, w1, g1)
    hq = mxq(h, 1, "e4m3")
    s1 = hq @ mxq(f64(v1), 0, "e4m3")
    p = (xq @ mxq(f64(wx), 0, "e4m3")) + (hq @ mxq(f64(wh), 0, "e4m3"))
    score = 0.8 * s1 + 0.8 * np.tanh(p)
    y = np.where(f64(u) < 0, -1.0, 1.0)
    return newton_target(y, score)


def e4m3fn_bytes(y):
    return np.clip(np.asarray(y, np.float64), -448.0, 448.0).astype(np.float32).astype(ml_dtypes.float8_e4m3fn).view(np.uint8)


def e4m3fn_values(b):
    return np.asarray(b, np.uint8).view(ml_dtypes.float8_e4m3fn).astype(np.float64)


def setup_inputs():
    d = draw0()
    x0 = np.asarray(d['x']).astype(np.float64)
    s = (np.max(np.abs(x0), axis=(0,), keepdims=True) / 448.0).astype(np.float32)
    out = {}
    for k, v in d.items():
        if k == 'x':
            out['x_bytes'] = e4m3fn_bytes(x0 / s.astype(np.float64))
            out['x_scale'] = s
        else:
            out[k] = v
    return out


def reference(x_bytes, x_scale, w1, g1, v1, wx, wh, u):
    return core(e4m3fn_values(x_bytes) * x_scale.astype(np.float64), w1, g1, v1, wx, wh, u)

@@ -1,0 +1,499 @@
+from contextlib import ExitStack
+
+import concourse.mybir as mybir
+from concourse.masks import make_identity
+
+B, D, H, C = 1024, 1024, 1024, 512
+FLOPS = 2 * B * D * H + 3 * 2 * B * D * C
+
+F32 = mybir.dt.float32
+BF16 = mybir.dt.bfloat16
+U32 = mybir.dt.uint32
+U8 = mybir.dt.uint8
+FP8 = mybir.dt.float8_e4m3fn
+FP8X4 = mybir.dt.float8_e4m3fn_x4
+ALU = mybir.AluOpType
+ACT = mybir.ActivationFunctionType
+
+P = 128
+LN2 = 0.6931471805599453
+
+
+def tile_grownetnewtontargets_kernel(tc, x_bytes, x_scale, w1, g1, v1, wx, wh, u, out):
+    nc = tc.nc
+    with ExitStack() as ctx:
+        keep = ctx.enter_context(tc.tile_pool(name="keep", bufs=1))
+        stage = ctx.enter_context(tc.tile_pool(name="stage", bufs=3))
+        psum = ctx.enter_context(tc.psum_pool(name="psum", bufs=8))
+        ctx.enter_context(tc.manual_schedule())
+
+        ident = keep.tile([P, P], F32, name="ident")
+        make_identity(nc, ident[:])
+
+        scale_cols = keep.tile([P, 8], F32, name="scale_cols")
+        nc.sync.dma_start(out=scale_cols[:], in_=x_scale.rearrange("o (p m) -> p (o m)", m=8))
+        ident_bf = keep.tile([P, P], BF16, name="ident_bf")
+        nc.gpsimd.tensor_copy(out=ident_bf[:], in_=ident[:])
+        warm = keep.tile([P, 1], F32, name="warm")
+        nc.vector.memset(warm[:], 0.0)
+        warm_out = keep.tile([P, 1], F32, name="warm_out")
+        nc.scalar.activation(out=warm_out[:], in_=warm[:], func=ACT.Tanh)
+
+        w1_raw = {}
+        w1_view = w1.rearrange("(g p j) n -> g p j n", p=P, j=4)
+
+        def load_w1(g, hg):
+            t = keep.tile([P, 4, 512], BF16, name=f"w1_raw_{g}_{hg}")
+            nc.sync.dma_start(out=t[:], in_=w1_view[g][:, :, hg * 512 : (hg + 1) * 512])
+            w1_raw[g, hg] = t
+
+        xb = {}
+        x_view = x_bytes.rearrange("(p j) k -> p j k", j=8)
+
+        def load_x(c):
+            t = keep.tile([P, 2, D], U8, name=f"xb_{c}")
+            nc.sync.dma_start(out=t[:], in_=x_view[:, 2 * c : 2 * c + 2, :])
+            xb[c] = t
+
+        w_raw = {}
+
+        def load_w(name, ap):
+            t = keep.tile([P, 2, 4, C], BF16, name=f"{name}_raw")
+            nc.sync.dma_start(out=t[:], in_=ap.rearrange("(g p j) c -> p g j c", p=P, j=4))
+            w_raw[name] = t
+
+        load_w1(0, 0)
+        load_x(0)
+        load_w1(1, 0)
+        load_x(1)
+        load_x(2)
+        load_w1(0, 1)
+        load_x(3)
+        load_w1(1, 1)
+        load_w("wx", wx)
+        load_w("v", v1)
+        load_w("wh", wh)
+        ub = keep.tile([P, 8, C], BF16, name="ub")
+        nc.sync.dma_start(out=ub[:], in_=u.rearrange("(p j) c -> p j c", j=8))
+        gain_bf = keep.tile([P, 2, 4], BF16, name="gain_bf")
+        nc.gpsimd.dma_start(out=gain_bf[:], in_=g1.rearrange("(g p t) -> p g t", p=P, t=4))
+        gain = keep.tile([P, 2, 4], F32, name="gain")
+        nc.gpsimd.tensor_copy(out=gain[:], in_=gain_bf[:])
+
+        scale = keep.tile([P, D], F32, name="scale")
+
+        spread = {}
+
+        def spread_scale(i):
+            bank = psum.tile([P, 4, P], F32, name="bank")
+            spread[i] = bank
+            for m in range(4):
+                column = scale_cols[:, 4 * i + m : 4 * i + m + 1]
+                nc.tensor.transpose(bank[:, m, :], column.to_broadcast([P, P]), ident[:])
+
+        def store_scale(engine, i):
+            d = scale[:].rearrange("q (p m) -> q p m", m=8)[:, :, 4 * i : 4 * i + 4]
+            s = spread[i][:].rearrange("q m p -> q p m")
+            if engine == "S":
+                nc.scalar.copy(out=d, in_=s)
+            else:
+                nc.vector.tensor_copy(out=d, in_=s)
+
+        w_codes = {}
+        w_scales = {}
+        w_grouped = {}
+
+        def inter(engine, key, piece):
+            if key not in w_grouped:
+                w_grouped[key] = stage.tile([P, 512, 4], BF16, name="wg", bufs=4, align_bytes=64)
+            dst = w_grouped[key]
+            if key[0] == "w1":
+                src = w1_raw[key[1], key[2]]
+                d = dst[:, 256 * piece : 256 * piece + 256, :].rearrange("p (t m) j -> p t m j", t=2)
+                s = src[:].rearrange("p j (m t) -> p t m j", t=4)[:, 2 * piece : 2 * piece + 2]
+            else:
+                cols = slice(piece * 256, (piece + 1) * 256)
+                d = dst[:, cols, :].rearrange("p (c i) t -> p c t i", i=4)
+                s = w_raw[key[0]][:, key[1], :, cols].rearrange("p t (c i) -> p c t i", i=4)
+            if engine == "S":
+                nc.scalar.copy(out=d, in_=s)
+            else:
+                nc.vector.tensor_copy(out=d, in_=s)
+
+        blends = {}
+
+        def blend(key, piece):
+            if key not in w_grouped:
+                w_grouped[key] = stage.tile([P, 512, 4], BF16, name="wg", bufs=4, align_bytes=64)
+            bank = psum.tile([P, 256, 4], BF16, name="bank")
+            for i in range(2):
+                if key[0] == "w1":
+                    s = w1_raw[key[1], key[2]][:].rearrange("p j (m t) -> p t m j", t=4)[:, 2 * piece + i]
+                else:
+                    c = 256 * piece + 128 * i
+                    s = w_raw[key[0]][:, key[1], :, c : c + 128].rearrange("p j c -> p c j")
+                nc.tensor.matmul(bank[:, 128 * i : 128 * i + 128, :], lhsT=ident_bf[:], rhs=s, start=True, stop=True)
+            blends[key, piece] = bank
+
+        def drain(engine, key, piece):
+            d = w_grouped[key][:, 256 * piece : 256 * piece + 256, :]
+            if engine == "S":
+                nc.scalar.copy(out=d, in_=blends[key, piece][:])
+            else:
+                nc.vector.tensor_copy(out=d, in_=blends[key, piece][:])
+
+        def quant_w(key):
+            tag = "_".join(str(k) for k in key)
+            codes = keep.tile([P, 512], U32, name=f"codes_{tag}", align_bytes=64)
+            scales = keep.tile([P, 512], U8, name=f"scales_{tag}", align_bytes=64)
+            nc.vector.quantize_mx(
+                out=codes[:].bitcast(FP8X4), scales=scales[:], in_=w_grouped[key][:].rearrange("p c t -> p (c t)")
+            )
+            w_codes[key] = codes
+            w_scales[key] = scales
+
+        xs = {}
+        xt = {}
+        xg = {}
+        x_codes = [keep.tile([P, 2, 512], U32, name=f"x_codes_{i}", align_bytes=64) for i in range(2)]
+        x_scales = [keep.tile([P, 2, 512], U8, name=f"x_scales_{i}", align_bytes=64) for i in range(2)]
+
+        def widen(j):
+            xs[j] = stage.tile([P, D], BF16, name="xs", bufs=4)
+            nc.vector.tensor_tensor(out=xs[j][:], in0=xb[j // 2][:, j % 2, :].bitcast(FP8), in1=scale[:], op=ALU.mult)
+
+        def turn(j):
+            words = xs[j][:].bitcast(F32)
+            xt[j] = psum.tile([P, 2, 2, P], F32, name="bank")
+            for g in range(2):
+                for e in range(2):
+                    nc.tensor.transpose(xt[j][:, g, e, :], words[:, 256 * g + e : 256 * (g + 1) : 2], ident[:])
+
+        def empty(engine, j):
+            c = j // 2
+            if j % 2 == 0:
+                xg[c] = stage.tile([P, 2, 256, 4], BF16, name="xg", bufs=2, align_bytes=64)
+            rows = slice((j % 2) * P, (j % 2 + 1) * P)
+            d, s = xg[c][:].bitcast(F32)[:, :, rows, :], xt[j][:].rearrange("p g e r -> p g r e")
+            if engine == "S":
+                nc.scalar.copy(out=d, in_=s)
+            else:
+                nc.vector.tensor_copy(out=d, in_=s)
+
+        def quant_x(c):
+            for g in range(2):
+                cols = slice((c % 2) * 256, (c % 2 + 1) * 256)
+                nc.vector.quantize_mx(
+                    out=x_codes[c // 2][:, g, cols].bitcast(FP8X4),
+                    scales=x_scales[c // 2][:, g, cols],
+                    in_=xg[c][:, g].rearrange("p r t -> p (r t)"),
+                )
+
+        def mx(acc, l_codes, l_scales, r_codes, r_scales, start, stop):
+            nc.tensor.matmul_mx(
+                out=acc, lhsT=l_codes.bitcast(FP8X4), lhsT_scale=l_scales, rhs=r_codes.bitcast(FP8X4), rhs_scale=r_scales,
+                start=start, stop=stop,
+            )
+
+        r = [keep.tile([P, 4, B], F32, name=f"r_{i}") for i in range(2)]
+        sums = [keep.tile([P, 2, 4], F32, name=f"sums_{i}") for i in range(2)]
+        mean = [keep.tile([P, 4], F32, name=f"mean_{i}") for i in range(2)]
+        shift = [keep.tile([P, 4], F32, name=f"shift_{i}") for i in range(2)]
+        hc = [keep.tile([P, 4, B], BF16, name=f"hc_{i}") for i in range(2)]
+        h_grouped = {}
+        h_codes = [keep.tile([P, B], U32, name=f"h_codes_{i}", align_bytes=64) for i in range(2)]
+        h_scales = [keep.tile([P, B], U8, name=f"h_scales_{i}", align_bytes=64) for i in range(2)]
+        acc1 = {}
+
+        def mm1(hg, half, t):
+            acc = psum.tile([P, 512], F32, name="bank")
+            for g in range(2):
+                cols = slice(t * P, (t + 1) * P)
+                key = ("w1", g, hg)
+                mx(acc[:], w_codes[key][:, cols], w_scales[key][:, cols], x_codes[half][:, g, :], x_scales[half][:, g, :], g == 0, g == 1)
+            acc1[hg, half, t] = acc
+
+        def relu(hg, half, t):
+            nc.scalar.activation(
+                out=r[hg][:, t, half * 512 : (half + 1) * 512], in_=acc1[hg, half, t][:], func=ACT.Relu,
+                accum_out=sums[hg][:, half, t : t + 1],
+            )
+
+        def means(hg):
+            total = stage.tile([P, 4], F32, name="total")
+            nc.vector.tensor_tensor(out=total[:], in0=sums[hg][:, 0, :], in1=sums[hg][:, 1, :], op=ALU.add)
+            nc.vector.tensor_scalar(out=mean[hg][:], in0=total[:], scalar1=1.0 / B, scalar2=None, op0=ALU.mult)
+            nc.vector.scalar_tensor_tensor(out=shift[hg][:], in0=mean[hg][:], scalar=-1.0, in1=gain[:, hg, :], op0=ALU.mult, op1=ALU.mult)
+
+        def center(engine, hg, half, t):
+            cols = slice(half * 512, (half + 1) * 512)
+            d, s = hc[hg][:, t, cols], r[hg][:, t, cols]
+            if engine == "S":
+                nc.scalar.activation(out=d, in_=s, func=ACT.Identity, scale=gain[:, hg, t : t + 1], bias=shift[hg][:, t : t + 1])
+            else:
+                nc.vector.tensor_scalar(
+                    out=d, in0=s, scalar1=mean[hg][:, t : t + 1], scalar2=gain[:, hg, t : t + 1],
+                    op0=ALU.subtract, op1=ALU.mult,
+                )
+
+        def inter_h(engine, hg, half):
+            t = stage.tile([P, 512, 4], BF16, name="hgrp", bufs=3, align_bytes=64)
+            h_grouped[hg, half] = t
+            d = t[:].rearrange("p (c i) t -> p c t i", i=4)
+            s = hc[hg][:, :, half * 512 : (half + 1) * 512].rearrange("p t (c i) -> p c t i", i=4)
+            if engine == "S":
+                nc.scalar.copy(out=d, in_=s)
+            else:
+                nc.vector.tensor_copy(out=d, in_=s)
+
+        def quant_h(hg, half):
+            cols = slice(half * 512, (half + 1) * 512)
+            nc.vector.quantize_mx(
+                out=h_codes[hg][:, cols].bitcast(FP8X4), scales=h_scales[hg][:, cols],
+                in_=h_grouped[hg, half][:].rearrange("p c t -> p (c t)"),
+            )
+
+        y_half = keep.tile([P, 8, C], BF16, name="y_half")
+        pb = {}
+        sb = {}
+
+        def sign(jj):
+            nc.vector.tensor_scalar(
+                out=y_half[:, 4 * jj : 4 * jj + 4, :], in0=ub[:, 4 * jj : 4 * jj + 4, :], scalar1=0.0, scalar2=0.5,
+                op0=ALU.is_ge, op1=ALU.subtract,
+            )
+
+        def x_cols(g, j):
+            return x_codes[j // 4][:, g, (j % 4) * P : (j % 4 + 1) * P], x_scales[j // 4][:, g, (j % 4) * P : (j % 4 + 1) * P]
+
+        def h_cols(hg, j):
+            return h_codes[hg][:, j * P : (j + 1) * P], h_scales[hg][:, j * P : (j + 1) * P]
+
+        def mm2_x(j):
+            pb[j] = psum.tile([P, C], F32, name="bank")
+            for g in range(2):
+                mx(pb[j][:], *x_cols(g, j), w_codes["wx", g][:], w_scales["wx", g][:], g == 0, False)
+
+        def mm2_h(j, hg):
+            if hg == 0:
+                sb[j] = psum.tile([P, C], F32, name="bank")
+            mx(pb[j][:], *h_cols(hg, j), w_codes["wh", hg][:], w_scales["wh", hg][:], False, hg == 1)
+            mx(sb[j][:], *h_cols(hg, j), w_codes["v", hg][:], w_scales["v", hg][:], hg == 0, hg == 1)
+
+        work = {}
+
+        def tanh(j):
+            work[j] = stage.tile([P, C], F32, name="work", bufs=6)
+            nc.scalar.activation(out=work[j][:], in_=pb[j][:], func=ACT.Tanh)
+
+        def add(j):
+            nc.vector.tensor_tensor(out=work[j][:], in0=sb[j][:], in1=work[j][:], op=ALU.add)
+
+        def margin(engine, j):
+            (nc.gpsimd if engine == "G" else nc.vector).tensor_tensor(out=work[j][:], in0=work[j][:], in1=y_half[:, j, :], op=ALU.mult)
+
+        def expo(j):
+            nc.scalar.activation(out=work[j][:], in_=work[j][:], func=ACT.Exp, scale=-1.6, bias=LN2)
+
+        def target(j):
+            nc.vector.scalar_tensor_tensor(
+                out=work[j][:], in0=work[j][:], scalar=2.0, in1=y_half[:, j, :], op0=ALU.add, op1=ALU.mult
+            )
+            nc.sync.dma_start(out=out.rearrange("(p j) c -> p j c", j=8)[:, j, :], in_=work[j][:])
+
+        inter("S", ("w1", 0, 0), 0)
+        spread_scale(0)
+        spread_scale(1)
+        store_scale("V", 0)
+        store_scale("V", 1)
+        widen(0)
+        blend(("w1", 0, 0), 1)
+        widen(1)
+        blend(("w1", 1, 0), 1)
+        blend(("w1", 1, 0), 0)
+        turn(0)
+        widen(2)
+        turn(1)
+        widen(3)
+        drain("S", ("w1", 0, 0), 1)
+        drain("S", ("w1", 1, 0), 0)
+        widen(4)
+        inter("S", ("w1", 0, 1), 0)
+        empty("S", 0)
+        widen(5)
+        drain("S", ("w1", 1, 0), 1)
+        blend(("w1", 0, 1), 1)
+        empty("S", 1)
+        turn(2)
+        turn(3)
+        empty("S", 2)
+        quant_w(("w1", 0, 0))
+        blend(("w1", 1, 1), 0)
+        turn(4)
+        quant_x(0)
+        drain("S", ("w1", 1, 1), 0)
+        turn(5)
+        widen(6)
+        empty("S", 3)
+        quant_w(("w1", 1, 0))
+        widen(7)
+        drain("S", ("w1", 0, 1), 1)
+        empty("S", 4)
+        blend(("wx", 0), 0)
+        quant_x(1)
+        empty("S", 5)
+        inter("S", ("wx", 1), 0)
+        turn(6)
+        drain("S", ("wx", 0), 0)
+        quant_w(("w1", 0, 1))
+        blend(("w1", 1, 1), 1)
+        drain("S", ("w1", 1, 1), 1)
+        quant_x(2)
+        turn(7)
+        quant_w(("w1", 1, 1))
+        mm1(0, 0, 0)
+        mm1(0, 0, 1)
+        mm1(0, 0, 2)
+        mm1(0, 0, 3)
+        empty("S", 6)
+        empty("S", 7)
+        quant_x(3)
+        mm1(0, 1, 0)
+        inter("V", ("v", 0), 0)
+        relu(0, 0, 0)
+        relu(0, 0, 1)
+        inter("V", ("wx", 1), 1)
+        relu(0, 0, 2)
+        relu(0, 0, 3)
+        mm1(1, 1, 0)
+        mm1(0, 1, 1)
+        relu(0, 1, 0)
+        mm1(0, 1, 2)
+        inter("V", ("wx", 0), 1)
+        mm1(0, 1, 3)
+        mm1(1, 0, 0)
+        quant_w(("wx", 1))
+        quant_w(("wx", 0))
+        sign(0)
+        relu(1, 1, 0)
+        relu(0, 1, 1)
+        relu(0, 1, 2)
+        inter("V", ("v", 0), 1)
+        relu(0, 1, 3)
+        relu(1, 0, 0)
+        mm1(1, 0, 1)
+        relu(1, 0, 1)
+        inter("V", ("wh", 0), 0)
+        mm1(1, 0, 2)
+        means(0)
+        inter("V", ("wh", 1), 0)
+        quant_w(("v", 0))
+        relu(1, 0, 2)
+        mm1(1, 1, 1)
+        center("V", 0, 0, 0)
+        relu(1, 1, 1)
+        mm1(1, 0, 3)
+        relu(1, 0, 3)
+        inter("V", ("wh", 0), 1)
+        center("S", 0, 0, 1)
+        blend(("wh", 1), 1)
+        center("V", 0, 0, 2)
+        mm1(1, 1, 2)
+        center("V", 0, 1, 0)
+        relu(1, 1, 2)
+        sign(1)
+        mm1(1, 1, 3)
+        drain("V", ("wh", 1), 1)
+        quant_w(("wh", 0))
+        center("S", 0, 0, 3)
+        relu(1, 1, 3)
+        means(1)
+        center("V", 1, 1, 0)
+        inter_h("S", 0, 0)
+        center("S", 1, 1, 1)
+        center("V", 1, 0, 0)
+        center("V", 0, 1, 1)
+        blend(("v", 1), 1)
+        center("V", 1, 0, 1)
+        quant_h(0, 0)
+        blend(("v", 1), 0)
+        center("S", 1, 0, 2)
+        drain("S", ("v", 1), 0)
+        mm2_x(0)
+        mm2_x(1)
+        center("V", 1, 0, 3)
+        mm2_x(2)
+        center("V", 0, 1, 2)
+        center("S", 0, 1, 3)
+        center("S", 1, 1, 2)
+        inter_h("V", 1, 0)
+        mm2_h(0, 0)
+        mm2_h(1, 0)
+        quant_w(("wh", 1))
+        mm2_x(3)
+        drain("S", ("v", 1), 1)
+        quant_h(1, 0)
+        quant_w(("v", 1))
+        mm2_h(2, 0)
+        center("S", 1, 1, 3)
+        inter_h("V", 1, 1)
+        mm2_x(4)
+        quant_h(1, 1)
+        inter_h("S", 0, 1)
+        mm2_h(0, 1)
+        mm2_h(1, 1)
+        tanh(0)
+        tanh(1)
+        mm2_h(2, 1)
+        mm2_h(3, 0)
+        mm2_h(3, 1)
+        tanh(2)
+        quant_h(0, 1)
+        add(0)
+        add(1)
+        mm2_h(4, 0)
+        mm2_x(5)
+        mm2_h(4, 1)
+        margin("V", 0)
+        mm2_h(5, 0)
+        expo(0)
+        margin("V", 1)
+        tanh(3)
+        mm2_h(5, 1)
+        expo(1)
+        add(2)
+        target(0)
+        add(3)
+        margin("V", 2)
+        target(1)
+        tanh(4)
+        expo(2)
+        tanh(5)
+        mm2_x(6)
+        mm2_x(7)
+        add(4)
+        target(2)
+        margin("V", 3)
+        mm2_h(6, 0)
+        expo(3)
+        mm2_h(6, 1)
+        tanh(6)
+        margin("V", 4)
+        add(5)
+        target(3)
+        expo(4)
+        mm2_h(7, 0)
+        margin("V", 5)
+        mm2_h(7, 1)
+        tanh(7)
+        target(4)
+        add(6)
+        add(7)
+        margin("V", 6)
+        expo(5)
+        target(5)
+        margin("V", 7)
+        expo(6)
+        expo(7)
+        target(6)
+        target(7)

@@ -109,8 +109,8 @@ def tile_grownetnewtontargets_kernel(tc, x_bytes, x_scale, w1, g1, v1, wx, wh, u
             dst = w_grouped[key]
             if key[0] == "w1":
                 src = w1_raw[key[1], key[2]]
-                d = dst[:, 256 * piece : 256 * piece + 256, :].rearrange("p (t m) j -> p t m j", t=2)
-                s = src[:].rearrange("p j (m t) -> p t m j", t=4)[:, 2 * piece : 2 * piece + 2]
+                d = dst[:].rearrange("p (t m) j -> p m j t", t=4)[:, piece * 64 : (piece + 1) * 64]
+                s = src[:].rearrange("p j (m t) -> p m j t", t=4)[:, piece * 64 : (piece + 1) * 64]
             else:
                 cols = slice(piece * 256, (piece + 1) * 256)
                 d = dst[:, cols, :].rearrange("p (c i) t -> p c t i", i=4)
@@ -301,196 +301,186 @@ def tile_grownetnewtontargets_kernel(tc, x_bytes, x_scale, w1, g1, v1, wx, wh, u
             )
             nc.sync.dma_start(out=out.rearrange("(p j) c -> p j c", j=8)[:, j, :], in_=work[j][:])
 
-        inter("S", ("w1", 0, 0), 0)
         spread_scale(0)
+        inter("S", ("w1", 0, 0), 0)
         spread_scale(1)
         store_scale("V", 0)
+        inter("S", ("w1", 0, 0), 1)
+        inter("S", ("w1", 1, 0), 0)
         store_scale("V", 1)
         widen(0)
-        blend(("w1", 0, 0), 1)
         widen(1)
-        blend(("w1", 1, 0), 1)
-        blend(("w1", 1, 0), 0)
-        turn(0)
         widen(2)
-        turn(1)
         widen(3)
-        drain("S", ("w1", 0, 0), 1)
-        drain("S", ("w1", 1, 0), 0)
-        widen(4)
-        inter("S", ("w1", 0, 1), 0)
+        turn(0)
+        inter("S", ("w1", 1, 0), 1)
+        turn(1)
         empty("S", 0)
-        widen(5)
-        drain("S", ("w1", 1, 0), 1)
-        blend(("w1", 0, 1), 1)
         empty("S", 1)
         turn(2)
-        turn(3)
+        widen(4)
+        inter("S", ("w1", 0, 1), 0)
+        inter("S", ("w1", 0, 1), 1)
+        widen(5)
         empty("S", 2)
+        inter("S", ("w1", 1, 1), 0)
         quant_w(("w1", 0, 0))
-        blend(("w1", 1, 1), 0)
-        turn(4)
+        turn(3)
         quant_x(0)
-        drain("S", ("w1", 1, 1), 0)
-        turn(5)
-        widen(6)
         empty("S", 3)
-        quant_w(("w1", 1, 0))
-        widen(7)
-        drain("S", ("w1", 0, 1), 1)
+        turn(4)
+        widen(6)
         empty("S", 4)
-        blend(("wx", 0), 0)
-        quant_x(1)
-        empty("S", 5)
+        turn(5)
+        inter("V", ("w1", 1, 1), 1)
+        quant_w(("w1", 1, 0))
         inter("S", ("wx", 1), 0)
-        turn(6)
-        drain("S", ("wx", 0), 0)
+        quant_x(1)
         quant_w(("w1", 0, 1))
-        blend(("w1", 1, 1), 1)
-        drain("S", ("w1", 1, 1), 1)
-        quant_x(2)
-        turn(7)
-        quant_w(("w1", 1, 1))
+        inter("S", ("v", 0), 0)
         mm1(0, 0, 0)
+        quant_w(("w1", 1, 1))
+        inter("V", ("wx", 1), 1)
+        inter("S", ("v", 0), 1)
+        turn(6)
         mm1(0, 0, 1)
+        widen(7)
+        inter("V", ("wh", 0), 0)
+        quant_w(("wx", 1))
+        relu(0, 0, 0)
+        empty("S", 5)
+        turn(7)
+        quant_x(2)
+        quant_w(("v", 0))
+        empty("S", 6)
+        mm1(1, 0, 0)
+        mm1(1, 0, 1)
+        empty("S", 7)
         mm1(0, 0, 2)
         mm1(0, 0, 3)
-        empty("S", 6)
-        empty("S", 7)
         quant_x(3)
-        mm1(0, 1, 0)
-        inter("V", ("v", 0), 0)
-        relu(0, 0, 0)
         relu(0, 0, 1)
-        inter("V", ("wx", 1), 1)
+        mm1(0, 1, 0)
+        mm1(0, 1, 1)
+        inter("V", ("wx", 0), 0)
+        inter("V", ("wh", 1), 0)
+        mm1(1, 1, 0)
+        inter("V", ("v", 1), 0)
+        relu(1, 0, 0)
         relu(0, 0, 2)
         relu(0, 0, 3)
-        mm1(1, 1, 0)
-        mm1(0, 1, 1)
-        relu(0, 1, 0)
-        mm1(0, 1, 2)
+        inter("V", ("wh", 0), 1)
+        relu(1, 0, 1)
         inter("V", ("wx", 0), 1)
-        mm1(0, 1, 3)
-        mm1(1, 0, 0)
-        quant_w(("wx", 1))
-        quant_w(("wx", 0))
-        sign(0)
+        relu(0, 1, 0)
+        inter("V", ("wh", 1), 1)
+        mm1(1, 1, 1)
+        mm1(0, 1, 2)
         relu(1, 1, 0)
+        quant_w(("wx", 0))
         relu(0, 1, 1)
         relu(0, 1, 2)
-        inter("V", ("v", 0), 1)
-        relu(0, 1, 3)
-        relu(1, 0, 0)
-        mm1(1, 0, 1)
-        relu(1, 0, 1)
-        inter("V", ("wh", 0), 0)
+        mm1(0, 1, 3)
         mm1(1, 0, 2)
-        means(0)
-        inter("V", ("wh", 1), 0)
-        quant_w(("v", 0))
-        relu(1, 0, 2)
-        mm1(1, 1, 1)
-        center("V", 0, 0, 0)
-        relu(1, 1, 1)
-        mm1(1, 0, 3)
-        relu(1, 0, 3)
-        inter("V", ("wh", 0), 1)
-        center("S", 0, 0, 1)
-        blend(("wh", 1), 1)
-        center("V", 0, 0, 2)
         mm1(1, 1, 2)
-        center("V", 0, 1, 0)
-        relu(1, 1, 2)
-        sign(1)
         mm1(1, 1, 3)
-        drain("V", ("wh", 1), 1)
-        quant_w(("wh", 0))
-        center("S", 0, 0, 3)
+        mm1(1, 0, 3)
+        relu(0, 1, 3)
+        relu(1, 1, 1)
+        inter("V", ("v", 1), 1)
+        mm2_x(0)
+        quant_w(("wh", 1))
+        relu(1, 0, 2)
+        relu(1, 1, 2)
+        means(0)
         relu(1, 1, 3)
+        center("V", 0, 0, 0)
+        center("V", 0, 0, 1)
+        quant_w(("wh", 0))
+        mm2_x(1)
+        relu(1, 0, 3)
+        quant_w(("v", 1))
+        center("S", 0, 0, 2)
+        center("S", 0, 0, 3)
         means(1)
-        center("V", 1, 1, 0)
-        inter_h("S", 0, 0)
-        center("S", 1, 1, 1)
         center("V", 1, 0, 0)
-        center("V", 0, 1, 1)
-        blend(("v", 1), 1)
+        inter_h("V", 0, 0)
         center("V", 1, 0, 1)
         quant_h(0, 0)
-        blend(("v", 1), 0)
-        center("S", 1, 0, 2)
-        drain("S", ("v", 1), 0)
-        mm2_x(0)
-        mm2_x(1)
-        center("V", 1, 0, 3)
         mm2_x(2)
-        center("V", 0, 1, 2)
-        center("S", 0, 1, 3)
-        center("S", 1, 1, 2)
-        inter_h("V", 1, 0)
+        center("S", 0, 1, 0)
         mm2_h(0, 0)
+        center("S", 0, 1, 1)
+        center("S", 1, 0, 2)
+        center("S", 1, 0, 3)
+        inter_h("V", 1, 0)
+        center("S", 0, 1, 2)
         mm2_h(1, 0)
-        quant_w(("wh", 1))
-        mm2_x(3)
-        drain("S", ("v", 1), 1)
-        quant_h(1, 0)
-        quant_w(("v", 1))
+        center("S", 0, 1, 3)
+        center("V", 1, 1, 0)
         mm2_h(2, 0)
-        center("S", 1, 1, 3)
-        inter_h("V", 1, 1)
-        mm2_x(4)
-        quant_h(1, 1)
+        quant_h(1, 0)
         inter_h("S", 0, 1)
+        center("V", 1, 1, 1)
         mm2_h(0, 1)
-        mm2_h(1, 1)
         tanh(0)
-        tanh(1)
+        sign(0)
+        mm2_h(1, 1)
+        center("V", 1, 1, 2)
+        sign(1)
+        mm2_x(3)
         mm2_h(2, 1)
+        center("V", 1, 1, 3)
+        tanh(1)
         mm2_h(3, 0)
-        mm2_h(3, 1)
-        tanh(2)
-        quant_h(0, 1)
+        inter_h("S", 1, 1)
         add(0)
         add(1)
-        mm2_h(4, 0)
-        mm2_x(5)
-        mm2_h(4, 1)
         margin("V", 0)
-        mm2_h(5, 0)
-        expo(0)
-        margin("V", 1)
+        mm2_x(4)
+        mm2_x(5)
+        quant_h(0, 1)
+        tanh(2)
+        mm2_h(3, 1)
         tanh(3)
-        mm2_h(5, 1)
-        expo(1)
+        margin("V", 1)
+        quant_h(1, 1)
+        expo(0)
         add(2)
-        target(0)
+        mm2_h(4, 0)
         add(3)
-        margin("V", 2)
-        target(1)
-        tanh(4)
-        expo(2)
-        tanh(5)
         mm2_x(6)
+        expo(1)
+        mm2_h(5, 0)
+        mm2_h(6, 0)
+        mm2_h(4, 1)
+        target(0)
+        mm2_h(5, 1)
+        margin("V", 2)
+        expo(2)
+        target(1)
+        margin("V", 3)
+        tanh(4)
+        mm2_h(6, 1)
+        tanh(5)
+        target(2)
+        expo(3)
+        tanh(6)
         mm2_x(7)
         add(4)
-        target(2)
-        margin("V", 3)
-        mm2_h(6, 0)
-        expo(3)
-        mm2_h(6, 1)
-        tanh(6)
-        margin("V", 4)
         add(5)
         target(3)
+        margin("V", 4)
+        add(6)
         expo(4)
         mm2_h(7, 0)
         margin("V", 5)
         mm2_h(7, 1)
         tanh(7)
+        expo(5)
         target(4)
-        add(6)
         add(7)
         margin("V", 6)
-        expo(5)
         target(5)
         margin("V", 7)
         expo(6)

@@ -102,55 +102,59 @@ def tile_grownetnewtontargets_kernel(tc, x_bytes, x_scale, w1, g1, v1, wx, wh, u
         w_codes = {}
         w_scales = {}
         w_grouped = {}
+        blends = {}
+
+        def grouped(key, piece):
+            if key[0] == "w1":
+                if key not in w_grouped:
+                    w_grouped[key] = stage.tile([P, 512, 4], BF16, name="w1g", bufs=3, align_bytes=64)
+                return w_grouped[key]
+            if (key, piece) not in w_grouped:
+                w_grouped[key, piece] = stage.tile([P, 256, 4], BF16, name="wg", bufs=6, align_bytes=64)
+            return w_grouped[key, piece]
 
         def inter(engine, key, piece):
-            if key not in w_grouped:
-                w_grouped[key] = stage.tile([P, 512, 4], BF16, name="wg", bufs=4, align_bytes=64)
-            dst = w_grouped[key]
+            dst = grouped(key, piece)
             if key[0] == "w1":
-                src = w1_raw[key[1], key[2]]
                 d = dst[:].rearrange("p (t m) j -> p m j t", t=4)[:, piece * 64 : (piece + 1) * 64]
-                s = src[:].rearrange("p j (m t) -> p m j t", t=4)[:, piece * 64 : (piece + 1) * 64]
+                s = w1_raw[key[1], key[2]][:].rearrange("p j (m t) -> p m j t", t=4)[:, piece * 64 : (piece + 1) * 64]
             else:
-                cols = slice(piece * 256, (piece + 1) * 256)
-                d = dst[:, cols, :].rearrange("p (c i) t -> p c t i", i=4)
-                s = w_raw[key[0]][:, key[1], :, cols].rearrange("p t (c i) -> p c t i", i=4)
+                d = dst[:].rearrange("p (c i) t -> p c t i", i=4)
+                s = w_raw[key[0]][:, key[1], :, piece * 256 : (piece + 1) * 256].rearrange("p t (c i) -> p c t i", i=4)
             if engine == "S":
                 nc.scalar.copy(out=d, in_=s)
             else:
                 nc.vector.tensor_copy(out=d, in_=s)
 
-        blends = {}
-
         def blend(key, piece):
-            if key not in w_grouped:
-                w_grouped[key] = stage.tile([P, 512, 4], BF16, name="wg", bufs=4, align_bytes=64)
             bank = psum.tile([P, 256, 4], BF16, name="bank")
             for i in range(2):
-                if key[0] == "w1":
-                    s = w1_raw[key[1], key[2]][:].rearrange("p j (m t) -> p t m j", t=4)[:, 2 * piece + i]
-                else:
-                    c = 256 * piece + 128 * i
-                    s = w_raw[key[0]][:, key[1], :, c : c + 128].rearrange("p j c -> p c j")
-                nc.tensor.matmul(bank[:, 128 * i : 128 * i + 128, :], lhsT=ident_bf[:], rhs=s, start=True, stop=True)
+                c = 256 * piece + 128 * i
+                nc.tensor.matmul(
+                    bank[:, 128 * i : 128 * i + 128, :].rearrange("p (c i) t -> p c t i", i=4),
+                    lhsT=ident_bf[:],
+                    rhs=w_raw[key[0]][:, key[1], :, c : c + 128].rearrange("p t (c i) -> p c t i", i=4),
+                    start=True, stop=True,
+                )
             blends[key, piece] = bank
 
         def drain(engine, key, piece):
-            d = w_grouped[key][:, 256 * piece : 256 * piece + 256, :]
+            d, s = grouped(key, piece)[:], blends[key, piece][:]
             if engine == "S":
-                nc.scalar.copy(out=d, in_=blends[key, piece][:])
+                nc.scalar.copy(out=d, in_=s)
             else:
-                nc.vector.tensor_copy(out=d, in_=blends[key, piece][:])
+                nc.vector.tensor_copy(out=d, in_=s)
 
-        def quant_w(key):
-            tag = "_".join(str(k) for k in key)
-            codes = keep.tile([P, 512], U32, name=f"codes_{tag}", align_bytes=64)
-            scales = keep.tile([P, 512], U8, name=f"scales_{tag}", align_bytes=64)
+        def quant_w(key, piece=None):
+            if key not in w_codes:
+                tag = "_".join(str(k) for k in key)
+                w_codes[key] = keep.tile([P, 512], U32, name=f"codes_{tag}", align_bytes=64)
+                w_scales[key] = keep.tile([P, 512], U8, name=f"scales_{tag}", align_bytes=64)
+            cols = slice(0, 512) if piece is None else slice(piece * 256, (piece + 1) * 256)
             nc.vector.quantize_mx(
-                out=codes[:].bitcast(FP8X4), scales=scales[:], in_=w_grouped[key][:].rearrange("p c t -> p (c t)")
+                out=w_codes[key][:, cols].bitcast(FP8X4), scales=w_scales[key][:, cols],
+                in_=grouped(key, piece)[:].rearrange("p c t -> p (c t)"),
             )
-            w_codes[key] = codes
-            w_scales[key] = scales
 
         xs = {}
         xt = {}
@@ -219,10 +223,16 @@ def tile_grownetnewtontargets_kernel(tc, x_bytes, x_scale, w1, g1, v1, wx, wh, u
                 accum_out=sums[hg][:, half, t : t + 1],
             )
 
-        def means(hg):
-            total = stage.tile([P, 4], F32, name="total")
-            nc.vector.tensor_tensor(out=total[:], in0=sums[hg][:, 0, :], in1=sums[hg][:, 1, :], op=ALU.add)
-            nc.vector.tensor_scalar(out=mean[hg][:], in0=total[:], scalar1=1.0 / B, scalar2=None, op0=ALU.mult)
+        totals = {}
+
+        def total(hg):
+            totals[hg] = stage.tile([P, 4], F32, name="total")
+            nc.vector.tensor_tensor(out=totals[hg][:], in0=sums[hg][:, 0, :], in1=sums[hg][:, 1, :], op=ALU.add)
+
+        def average(hg):
+            nc.vector.tensor_scalar(out=mean[hg][:], in0=totals[hg][:], scalar1=1.0 / B, scalar2=None, op0=ALU.mult)
+
+        def offset(hg):
             nc.vector.scalar_tensor_tensor(out=shift[hg][:], in0=mean[hg][:], scalar=-1.0, in1=gain[:, hg, :], op0=ALU.mult, op1=ALU.mult)
 
         def center(engine, hg, half, t):
@@ -254,13 +264,14 @@ def tile_grownetnewtontargets_kernel(tc, x_bytes, x_scale, w1, g1, v1, wx, wh, u
             )
 
         y_half = keep.tile([P, 8, C], BF16, name="y_half")
+        units = [(2 * (k % 4), 2, k // 4) for k in range(7)] + [(6, 1, 1), (7, 1, 1)]
         pb = {}
         sb = {}
 
-        def sign(jj):
+        def sign(jp):
+            js = slice(2 * jp, 2 * jp + 2)
             nc.vector.tensor_scalar(
-                out=y_half[:, 4 * jj : 4 * jj + 4, :], in0=ub[:, 4 * jj : 4 * jj + 4, :], scalar1=0.0, scalar2=0.5,
-                op0=ALU.is_ge, op1=ALU.subtract,
+                out=y_half[:, js, :], in0=ub[:, js, :], scalar1=0.0, scalar2=0.5, op0=ALU.is_ge, op1=ALU.subtract
             )
 
         def x_cols(g, j):
@@ -269,221 +280,253 @@ def tile_grownetnewtontargets_kernel(tc, x_bytes, x_scale, w1, g1, v1, wx, wh, u
         def h_cols(hg, j):
             return h_codes[hg][:, j * P : (j + 1) * P], h_scales[hg][:, j * P : (j + 1) * P]
 
-        def mm2_x(j):
-            pb[j] = psum.tile([P, C], F32, name="bank")
-            for g in range(2):
-                mx(pb[j][:], *x_cols(g, j), w_codes["wx", g][:], w_scales["wx", g][:], g == 0, False)
+        def mm2_p(k):
+            j0, nj, ch = units[k]
+            cols = slice(ch * 256, (ch + 1) * 256)
+            pb[k] = psum.tile([P, nj, 256], F32, name="bank")
+            for i in range(nj):
+                for g in range(2):
+                    mx(pb[k][:, i, :], *x_cols(g, j0 + i), w_codes["wx", g][:, cols], w_scales["wx", g][:, cols], g == 0, False)
+                for g in range(2):
+                    mx(pb[k][:, i, :], *h_cols(g, j0 + i), w_codes["wh", g][:, cols], w_scales["wh", g][:, cols], False, g == 1)
 
-        def mm2_h(j, hg):
-            if hg == 0:
-                sb[j] = psum.tile([P, C], F32, name="bank")
-            mx(pb[j][:], *h_cols(hg, j), w_codes["wh", hg][:], w_scales["wh", hg][:], False, hg == 1)
-            mx(sb[j][:], *h_cols(hg, j), w_codes["v", hg][:], w_scales["v", hg][:], hg == 0, hg == 1)
+        def mm2_s(k):
+            j0, nj, ch = units[k]
+            cols = slice(ch * 256, (ch + 1) * 256)
+            sb[k] = psum.tile([P, nj, 256], F32, name="bank")
+            for i in range(nj):
+                for g in range(2):
+                    mx(sb[k][:, i, :], *h_cols(g, j0 + i), w_codes["v", g][:, cols], w_scales["v", g][:, cols], g == 0, g == 1)
 
         work = {}
 
-        def tanh(j):
-            work[j] = stage.tile([P, C], F32, name="work", bufs=6)
-            nc.scalar.activation(out=work[j][:], in_=pb[j][:], func=ACT.Tanh)
+        def y_of(k):
+            j0, nj, ch = units[k]
+            return y_half[:, j0 : j0 + nj, ch * 256 : (ch + 1) * 256]
 
-        def add(j):
-            nc.vector.tensor_tensor(out=work[j][:], in0=sb[j][:], in1=work[j][:], op=ALU.add)
+        def tanh(k):
+            work[k] = stage.tile([P, units[k][1], 256], F32, name="work", bufs=6)
+            nc.scalar.activation(out=work[k][:], in_=pb[k][:], func=ACT.Tanh)
 
-        def margin(engine, j):
-            (nc.gpsimd if engine == "G" else nc.vector).tensor_tensor(out=work[j][:], in0=work[j][:], in1=y_half[:, j, :], op=ALU.mult)
+        def add(k):
+            nc.vector.tensor_tensor(out=work[k][:], in0=sb[k][:], in1=work[k][:], op=ALU.add)
 
-        def expo(j):
-            nc.scalar.activation(out=work[j][:], in_=work[j][:], func=ACT.Exp, scale=-1.6, bias=LN2)
+        def margin(engine, k):
+            (nc.gpsimd if engine == "G" else nc.vector).tensor_tensor(out=work[k][:], in0=work[k][:], in1=y_of(k), op=ALU.mult)
 
-        def target(j):
+        def expo(k):
+            nc.scalar.activation(out=work[k][:], in_=work[k][:], func=ACT.Exp, scale=-1.6, bias=LN2)
+
+        def target(k):
+            j0, nj, ch = units[k]
             nc.vector.scalar_tensor_tensor(
-                out=work[j][:], in0=work[j][:], scalar=2.0, in1=y_half[:, j, :], op0=ALU.add, op1=ALU.mult
+                out=work[k][:], in0=work[k][:], scalar=2.0, in1=y_of(k), op0=ALU.add, op1=ALU.mult
             )
-            nc.sync.dma_start(out=out.rearrange("(p j) c -> p j c", j=8)[:, j, :], in_=work[j][:])
+            nc.sync.dma_start(
+                out=out.rearrange("(p j) c -> p j c", j=8)[:, j0 : j0 + nj, ch * 256 : (ch + 1) * 256], in_=work[k][:]
+            )
 
+        inter("V", ("w1", 0, 0), 0)
         spread_scale(0)
-        inter("S", ("w1", 0, 0), 0)
+        store_scale("S", 0)
         spread_scale(1)
-        store_scale("V", 0)
-        inter("S", ("w1", 0, 0), 1)
-        inter("S", ("w1", 1, 0), 0)
         store_scale("V", 1)
         widen(0)
+        inter("S", ("w1", 0, 0), 1)
         widen(1)
-        widen(2)
-        widen(3)
         turn(0)
-        inter("S", ("w1", 1, 0), 1)
+        quant_w(("w1", 0, 0))
         turn(1)
+        widen(2)
+        inter("S", ("w1", 1, 0), 0)
+        widen(3)
+        inter("S", ("w1", 1, 0), 1)
+        widen(4)
+        widen(5)
         empty("S", 0)
         empty("S", 1)
-        turn(2)
-        widen(4)
-        inter("S", ("w1", 0, 1), 0)
-        inter("S", ("w1", 0, 1), 1)
-        widen(5)
-        empty("S", 2)
-        inter("S", ("w1", 1, 1), 0)
-        quant_w(("w1", 0, 0))
-        turn(3)
         quant_x(0)
+        turn(2)
+        inter("S", ("w1", 0, 1), 0)
+        empty("S", 2)
+        turn(3)
+        inter("S", ("w1", 1, 1), 0)
+        widen(6)
         empty("S", 3)
         turn(4)
-        widen(6)
-        empty("S", 4)
-        turn(5)
-        inter("V", ("w1", 1, 1), 1)
-        quant_w(("w1", 1, 0))
-        inter("S", ("wx", 1), 0)
+        inter("S", ("w1", 1, 1), 1)
+        widen(7)
         quant_x(1)
-        quant_w(("w1", 0, 1))
+        blend(("wx", 1), 0)
+        turn(5)
+        blend(("wx", 0), 0)
+        turn(6)
+        drain("S", ("wx", 1), 0)
+        empty("S", 4)
+        quant_w(("w1", 1, 0))
+        turn(7)
+        drain("V", ("wx", 0), 0)
         inter("S", ("v", 0), 0)
         mm1(0, 0, 0)
-        quant_w(("w1", 1, 1))
-        inter("V", ("wx", 1), 1)
-        inter("S", ("v", 0), 1)
-        turn(6)
-        mm1(0, 0, 1)
-        widen(7)
-        inter("V", ("wh", 0), 0)
-        quant_w(("wx", 1))
-        relu(0, 0, 0)
+        inter("V", ("w1", 0, 1), 1)
         empty("S", 5)
-        turn(7)
         quant_x(2)
-        quant_w(("v", 0))
         empty("S", 6)
-        mm1(1, 0, 0)
-        mm1(1, 0, 1)
-        empty("S", 7)
+        mm1(0, 0, 1)
         mm1(0, 0, 2)
         mm1(0, 0, 3)
+        empty("S", 7)
+        relu(0, 0, 0)
         quant_x(3)
+        quant_w(("w1", 0, 1))
+        sign(0)
         relu(0, 0, 1)
+        inter("V", ("wh", 1), 0)
         mm1(0, 1, 0)
         mm1(0, 1, 1)
-        inter("V", ("wx", 0), 0)
-        inter("V", ("wh", 1), 0)
-        mm1(1, 1, 0)
-        inter("V", ("v", 1), 0)
-        relu(1, 0, 0)
+        mm1(0, 1, 2)
         relu(0, 0, 2)
         relu(0, 0, 3)
-        inter("V", ("wh", 0), 1)
-        relu(1, 0, 1)
-        inter("V", ("wx", 0), 1)
-        relu(0, 1, 0)
-        inter("V", ("wh", 1), 1)
-        mm1(1, 1, 1)
-        mm1(0, 1, 2)
-        relu(1, 1, 0)
-        quant_w(("wx", 0))
-        relu(0, 1, 1)
-        relu(0, 1, 2)
+        quant_w(("w1", 1, 1))
         mm1(0, 1, 3)
+        mm1(1, 1, 0)
+        relu(0, 1, 0)
+        mm1(1, 1, 1)
+        inter("V", ("wh", 1), 1)
+        mm1(1, 0, 0)
+        sign(1)
+        relu(0, 1, 1)
+        mm1(1, 0, 1)
+        inter("V", ("wh", 0), 0)
+        relu(0, 1, 2)
         mm1(1, 0, 2)
+        relu(0, 1, 3)
+        quant_w(("v", 0), 0)
+        total(0)
+        quant_w(("wx", 0), 0)
+        average(0)
+        quant_w(("wx", 1), 0)
+        center("V", 0, 0, 0)
+        relu(1, 1, 0)
+        mm1(1, 0, 3)
+        center("V", 0, 0, 1)
+        relu(1, 1, 1)
+        center("V", 0, 0, 2)
+        relu(1, 0, 0)
         mm1(1, 1, 2)
         mm1(1, 1, 3)
-        mm1(1, 0, 3)
-        relu(0, 1, 3)
-        relu(1, 1, 1)
-        inter("V", ("v", 1), 1)
-        mm2_x(0)
-        quant_w(("wh", 1))
+        sign(2)
+        relu(1, 0, 1)
         relu(1, 0, 2)
-        relu(1, 1, 2)
-        means(0)
-        relu(1, 1, 3)
-        center("V", 0, 0, 0)
-        center("V", 0, 0, 1)
-        quant_w(("wh", 0))
-        mm2_x(1)
         relu(1, 0, 3)
-        quant_w(("v", 1))
-        center("S", 0, 0, 2)
-        center("S", 0, 0, 3)
-        means(1)
-        center("V", 1, 0, 0)
+        relu(1, 1, 2)
+        center("V", 0, 0, 3)
+        relu(1, 1, 3)
+        offset(0)
+        quant_w(("wh", 0), 0)
+        center("V", 0, 1, 0)
+        blend(("v", 1), 0)
         inter_h("V", 0, 0)
-        center("V", 1, 0, 1)
-        quant_h(0, 0)
-        mm2_x(2)
-        center("S", 0, 1, 0)
-        mm2_h(0, 0)
-        center("S", 0, 1, 1)
-        center("S", 1, 0, 2)
-        center("S", 1, 0, 3)
-        inter_h("V", 1, 0)
+        center("V", 0, 1, 1)
+        blend(("v", 1), 1)
         center("S", 0, 1, 2)
-        mm2_h(1, 0)
+        total(1)
         center("S", 0, 1, 3)
-        center("V", 1, 1, 0)
-        mm2_h(2, 0)
+        quant_w(("wh", 1), 0)
+        blend(("wh", 0), 1)
+        average(1)
+        blend(("wx", 1), 1)
+        quant_h(0, 0)
+        offset(1)
+        blend(("wx", 0), 1)
+        center("V", 1, 0, 0)
+        drain("S", ("v", 1), 0)
+        center("S", 1, 0, 1)
+        center("S", 1, 1, 0)
+        center("S", 1, 1, 1)
+        center("V", 1, 0, 2)
+        center("V", 1, 0, 3)
+        center("S", 1, 1, 2)
+        center("V", 1, 1, 3)
+        inter_h("V", 1, 0)
         quant_h(1, 0)
         inter_h("S", 0, 1)
-        center("V", 1, 1, 1)
-        mm2_h(0, 1)
+        inter_h("V", 1, 1)
+        mm2_p(0)
         tanh(0)
-        sign(0)
-        mm2_h(1, 1)
-        center("V", 1, 1, 2)
-        sign(1)
-        mm2_x(3)
-        mm2_h(2, 1)
-        center("V", 1, 1, 3)
-        tanh(1)
-        mm2_h(3, 0)
-        inter_h("S", 1, 1)
-        add(0)
-        add(1)
-        margin("V", 0)
-        mm2_x(4)
-        mm2_x(5)
-        quant_h(0, 1)
-        tanh(2)
-        mm2_h(3, 1)
-        tanh(3)
-        margin("V", 1)
+        mm2_p(1)
+        quant_w(("v", 1), 0)
+        mm2_s(0)
+        drain("S", ("v", 1), 1)
         quant_h(1, 1)
-        expo(0)
+        quant_h(0, 1)
+        drain("S", ("wh", 0), 1)
+        quant_w(("wh", 1), 1)
+        mm2_p(2)
+        mm2_s(1)
+        quant_w(("v", 1), 1)
+        add(0)
+        quant_w(("wh", 0), 1)
+        drain("S", ("wx", 0), 1)
+        drain("S", ("wx", 1), 1)
+        mm2_s(2)
+        tanh(1)
+        quant_w(("wx", 0), 1)
+        sign(3)
+        tanh(2)
+        quant_w(("wx", 1), 1)
+        add(1)
+        margin("G", 0)
+        inter("S", ("v", 0), 1)
         add(2)
-        mm2_h(4, 0)
-        add(3)
-        mm2_x(6)
+        mm2_p(3)
+        mm2_s(3)
+        margin("V", 1)
+        expo(0)
         expo(1)
-        mm2_h(5, 0)
-        mm2_h(6, 0)
-        mm2_h(4, 1)
-        target(0)
-        mm2_h(5, 1)
+        tanh(3)
         margin("V", 2)
-        expo(2)
+        quant_w(("v", 0), 1)
+        target(0)
+        mm2_p(4)
+        mm2_p(5)
         target(1)
-        margin("V", 3)
+        expo(2)
+        mm2_s(4)
+        add(3)
+        mm2_s(5)
         tanh(4)
-        mm2_h(6, 1)
         tanh(5)
         target(2)
+        margin("G", 3)
         expo(3)
-        tanh(6)
-        mm2_x(7)
         add(4)
+        mm2_p(6)
+        mm2_s(6)
         add(5)
-        target(3)
         margin("V", 4)
+        tanh(6)
+        margin("V", 5)
+        target(3)
+        mm2_s(7)
+        mm2_p(7)
         add(6)
         expo(4)
-        mm2_h(7, 0)
-        margin("V", 5)
-        mm2_h(7, 1)
-        tanh(7)
-        expo(5)
+        mm2_s(8)
         target(4)
-        add(7)
+        expo(5)
         margin("V", 6)
         target(5)
-        margin("V", 7)
+        tanh(7)
+        mm2_p(8)
+        tanh(8)
+        add(7)
+        add(8)
         expo(6)
-        expo(7)
         target(6)
+        margin("V", 7)
+        margin("V", 8)
+        expo(7)
         target(7)
+        expo(8)
+        target(8)

@@ -264,12 +264,18 @@ def tile_grownetnewtontargets_kernel(tc, x_bytes, x_scale, w1, g1, v1, wx, wh, u
             )
 
         y_half = keep.tile([P, 8, C], BF16, name="y_half")
-        units = [(2 * (k % 4), 2, k // 4) for k in range(7)] + [(6, 1, 1), (7, 1, 1)]
+        units = [(k, 0, C) for k in range(7)] + [(7, 0, C // 2), (7, C // 2, C)]
         pb = {}
         sb = {}
 
-        def sign(jp):
+        y_size = {}
+
+        def sign(engine, jp):
             js = slice(2 * jp, 2 * jp + 2)
+            y_size[2 * jp] = y_size[2 * jp + 1] = 1.0 if engine == "S" else 0.5
+            if engine == "S":
+                nc.scalar.activation(out=y_half[:, js, :], in_=ub[:, js, :], func=ACT.Sign, scale=2.0**20, bias=2.0**-120)
+                return
             nc.vector.tensor_scalar(
                 out=y_half[:, js, :], in0=ub[:, js, :], scalar1=0.0, scalar2=0.5, op0=ALU.is_ge, op1=ALU.subtract
             )
@@ -280,32 +286,28 @@ def tile_grownetnewtontargets_kernel(tc, x_bytes, x_scale, w1, g1, v1, wx, wh, u
         def h_cols(hg, j):
             return h_codes[hg][:, j * P : (j + 1) * P], h_scales[hg][:, j * P : (j + 1) * P]
 
-        def mm2_p(k):
-            j0, nj, ch = units[k]
-            cols = slice(ch * 256, (ch + 1) * 256)
-            pb[k] = psum.tile([P, nj, 256], F32, name="bank")
-            for i in range(nj):
-                for g in range(2):
-                    mx(pb[k][:, i, :], *x_cols(g, j0 + i), w_codes["wx", g][:, cols], w_scales["wx", g][:, cols], g == 0, False)
-                for g in range(2):
-                    mx(pb[k][:, i, :], *h_cols(g, j0 + i), w_codes["wh", g][:, cols], w_scales["wh", g][:, cols], False, g == 1)
+        def mm2_x(k):
+            j, lo, hi = units[k]
+            pb[k] = psum.tile([P, hi - lo], F32, name="bank")
+            for g in range(2):
+                mx(pb[k][:], *x_cols(g, j), w_codes["wx", g][:, lo:hi], w_scales["wx", g][:, lo:hi], g == 0, False)
 
-        def mm2_s(k):
-            j0, nj, ch = units[k]
-            cols = slice(ch * 256, (ch + 1) * 256)
-            sb[k] = psum.tile([P, nj, 256], F32, name="bank")
-            for i in range(nj):
-                for g in range(2):
-                    mx(sb[k][:, i, :], *h_cols(g, j0 + i), w_codes["v", g][:, cols], w_scales["v", g][:, cols], g == 0, g == 1)
+        def mm2_h(k, hg):
+            j, lo, hi = units[k]
+            if hg == 0:
+                sb[k] = psum.tile([P, hi - lo], F32, name="bank")
+            mx(pb[k][:], *h_cols(hg, j), w_codes["wh", hg][:, lo:hi], w_scales["wh", hg][:, lo:hi], False, hg == 1)
+            mx(sb[k][:], *h_cols(hg, j), w_codes["v", hg][:, lo:hi], w_scales["v", hg][:, lo:hi], hg == 0, hg == 1)
 
         work = {}
 
         def y_of(k):
-            j0, nj, ch = units[k]
-            return y_half[:, j0 : j0 + nj, ch * 256 : (ch + 1) * 256]
+            j, lo, hi = units[k]
+            return y_half[:, j, lo:hi]
 
         def tanh(k):
-            work[k] = stage.tile([P, units[k][1], 256], F32, name="work", bufs=6)
+            j, lo, hi = units[k]
+            work[k] = stage.tile([P, hi - lo], F32, name="work", bufs=6)
             nc.scalar.activation(out=work[k][:], in_=pb[k][:], func=ACT.Tanh)
 
         def add(k):
@@ -315,218 +317,224 @@ def tile_grownetnewtontargets_kernel(tc, x_bytes, x_scale, w1, g1, v1, wx, wh, u
             (nc.gpsimd if engine == "G" else nc.vector).tensor_tensor(out=work[k][:], in0=work[k][:], in1=y_of(k), op=ALU.mult)
 
         def expo(k):
-            nc.scalar.activation(out=work[k][:], in_=work[k][:], func=ACT.Exp, scale=-1.6, bias=LN2)
+            size = y_size[units[k][0]]
+            nc.scalar.activation(
+                out=work[k][:], in_=work[k][:], func=ACT.Exp, scale=-0.8 / size, bias=0.0 if size == 1.0 else LN2
+            )
 
         def target(k):
-            j0, nj, ch = units[k]
+            j, lo, hi = units[k]
             nc.vector.scalar_tensor_tensor(
-                out=work[k][:], in0=work[k][:], scalar=2.0, in1=y_of(k), op0=ALU.add, op1=ALU.mult
+                out=work[k][:], in0=work[k][:], scalar=1.0 / y_size[j], in1=y_of(k), op0=ALU.add, op1=ALU.mult
             )
-            nc.sync.dma_start(
-                out=out.rearrange("(p j) c -> p j c", j=8)[:, j0 : j0 + nj, ch * 256 : (ch + 1) * 256], in_=work[k][:]
-            )
+            nc.sync.dma_start(out=out.rearrange("(p j) c -> p j c", j=8)[:, j, lo:hi], in_=work[k][:])
 
-        inter("V", ("w1", 0, 0), 0)
+        inter("S", ("w1", 0, 0), 0)
+        inter("V", ("w1", 0, 0), 1)
         spread_scale(0)
-        store_scale("S", 0)
         spread_scale(1)
-        store_scale("V", 1)
-        widen(0)
-        inter("S", ("w1", 0, 0), 1)
-        widen(1)
-        turn(0)
-        quant_w(("w1", 0, 0))
-        turn(1)
-        widen(2)
+        store_scale("V", 0)
+        store_scale("S", 1)
         inter("S", ("w1", 1, 0), 0)
-        widen(3)
         inter("S", ("w1", 1, 0), 1)
-        widen(4)
-        widen(5)
-        empty("S", 0)
-        empty("S", 1)
-        quant_x(0)
-        turn(2)
+        quant_w(("w1", 0, 0))
         inter("S", ("w1", 0, 1), 0)
-        empty("S", 2)
-        turn(3)
+        widen(0)
+        turn(0)
+        empty("S", 0)
+        widen(1)
+        inter("S", ("w1", 0, 1), 1)
+        widen(2)
         inter("S", ("w1", 1, 1), 0)
-        widen(6)
-        empty("S", 3)
+        turn(1)
+        turn(2)
+        empty("S", 1)
+        widen(3)
+        widen(4)
+        turn(3)
         turn(4)
-        inter("S", ("w1", 1, 1), 1)
-        widen(7)
-        quant_x(1)
-        blend(("wx", 1), 0)
+        empty("S", 2)
+        blend(("wx", 0), 1)
+        widen(5)
+        empty("S", 3)
         turn(5)
-        blend(("wx", 0), 0)
-        turn(6)
-        drain("S", ("wx", 1), 0)
-        empty("S", 4)
+        widen(6)
+        widen(7)
+        quant_x(0)
+        inter("S", ("wx", 0), 0)
         quant_w(("w1", 1, 0))
-        turn(7)
-        drain("V", ("wx", 0), 0)
-        inter("S", ("v", 0), 0)
-        mm1(0, 0, 0)
-        inter("V", ("w1", 0, 1), 1)
+        quant_x(1)
+        inter("V", ("wx", 1), 0)
+        inter("S", ("w1", 1, 1), 1)
+        empty("S", 4)
+        turn(6)
         empty("S", 5)
-        quant_x(2)
-        empty("S", 6)
+        quant_w(("w1", 0, 1))
+        quant_w(("w1", 1, 1))
+        turn(7)
+        inter("V", ("wx", 1), 1)
+        blend(("v", 1), 0)
+        mm1(0, 0, 0)
         mm1(0, 0, 1)
         mm1(0, 0, 2)
-        mm1(0, 0, 3)
+        empty("S", 6)
         empty("S", 7)
+        drain("S", ("wx", 0), 1)
+        mm1(0, 0, 3)
+        quant_x(2)
+        mm1(1, 0, 0)
+        drain("S", ("v", 1), 0)
         relu(0, 0, 0)
         quant_x(3)
-        quant_w(("w1", 0, 1))
-        sign(0)
-        relu(0, 0, 1)
-        inter("V", ("wh", 1), 0)
-        mm1(0, 1, 0)
-        mm1(0, 1, 1)
-        mm1(0, 1, 2)
-        relu(0, 0, 2)
-        relu(0, 0, 3)
-        quant_w(("w1", 1, 1))
-        mm1(0, 1, 3)
-        mm1(1, 1, 0)
-        relu(0, 1, 0)
-        mm1(1, 1, 1)
-        inter("V", ("wh", 1), 1)
-        mm1(1, 0, 0)
-        sign(1)
-        relu(0, 1, 1)
-        mm1(1, 0, 1)
-        inter("V", ("wh", 0), 0)
-        relu(0, 1, 2)
-        mm1(1, 0, 2)
-        relu(0, 1, 3)
-        quant_w(("v", 0), 0)
-        total(0)
-        quant_w(("wx", 0), 0)
-        average(0)
         quant_w(("wx", 1), 0)
-        center("V", 0, 0, 0)
-        relu(1, 1, 0)
-        mm1(1, 0, 3)
-        center("V", 0, 0, 1)
-        relu(1, 1, 1)
-        center("V", 0, 0, 2)
+        relu(0, 0, 1)
+        mm1(0, 1, 0)
+        quant_w(("wx", 0), 0)
+        quant_w(("wx", 1), 1)
+        mm1(0, 1, 1)
+        quant_w(("v", 1), 0)
+        mm1(0, 1, 2)
+        sign("V", 0)
+        mm1(0, 1, 3)
+        relu(0, 0, 2)
+        inter("V", ("wh", 1), 0)
+        inter("V", ("v", 0), 0)
+        mm1(1, 0, 1)
+        mm1(1, 0, 2)
+        relu(0, 0, 3)
+        quant_w(("wx", 0), 1)
+        relu(0, 1, 0)
+        relu(0, 1, 1)
+        relu(0, 1, 2)
+        relu(0, 1, 3)
+        inter("V", ("v", 0), 1)
         relu(1, 0, 0)
-        mm1(1, 1, 2)
-        mm1(1, 1, 3)
-        sign(2)
+        quant_w(("v", 0), 0)
+        mm1(1, 1, 0)
+        inter("V", ("wh", 0), 0)
+        mm1(1, 1, 1)
+        total(0)
+        quant_w(("wh", 1), 0)
         relu(1, 0, 1)
         relu(1, 0, 2)
-        relu(1, 0, 3)
-        relu(1, 1, 2)
-        center("V", 0, 0, 3)
-        relu(1, 1, 3)
-        offset(0)
+        relu(1, 1, 0)
+        mm1(1, 1, 2)
         quant_w(("wh", 0), 0)
-        center("V", 0, 1, 0)
-        blend(("v", 1), 0)
-        inter_h("V", 0, 0)
-        center("V", 0, 1, 1)
+        average(0)
+        inter("V", ("wh", 0), 1)
+        center("V", 0, 0, 0)
+        mm1(1, 1, 3)
+        center("V", 0, 0, 1)
+        mm1(1, 0, 3)
         blend(("v", 1), 1)
-        center("S", 0, 1, 2)
+        relu(1, 1, 1)
+        mm2_x(0)
+        center("V", 0, 0, 2)
+        mm2_x(1)
+        center("V", 0, 0, 3)
+        offset(0)
+        quant_w(("wh", 0), 1)
+        relu(1, 1, 2)
+        relu(1, 1, 3)
+        relu(1, 0, 3)
+        inter("S", ("wh", 1), 1)
+        inter_h("V", 0, 0)
+        quant_w(("v", 0), 1)
         total(1)
-        center("S", 0, 1, 3)
-        quant_w(("wh", 1), 0)
-        blend(("wh", 0), 1)
-        average(1)
-        blend(("wx", 1), 1)
+        center("S", 0, 1, 0)
+        mm2_x(2)
         quant_h(0, 0)
+        average(1)
+        center("V", 0, 1, 1)
+        center("V", 0, 1, 2)
+        drain("S", ("v", 1), 1)
         offset(1)
-        blend(("wx", 0), 1)
         center("V", 1, 0, 0)
-        drain("S", ("v", 1), 0)
-        center("S", 1, 0, 1)
-        center("S", 1, 1, 0)
-        center("S", 1, 1, 1)
+        mm2_h(0, 0)
+        center("V", 1, 0, 1)
         center("V", 1, 0, 2)
-        center("V", 1, 0, 3)
-        center("S", 1, 1, 2)
-        center("V", 1, 1, 3)
+        quant_w(("wh", 1), 1)
+        center("S", 1, 0, 3)
+        center("S", 1, 1, 0)
+        mm2_h(1, 0)
+        mm2_x(3)
+        center("V", 1, 1, 1)
         inter_h("V", 1, 0)
+        quant_w(("v", 1), 1)
+        center("S", 0, 1, 3)
+        mm2_h(2, 0)
         quant_h(1, 0)
+        mm2_h(3, 0)
+        center("V", 1, 1, 2)
+        center("S", 1, 1, 3)
+        sign("V", 1)
+        mm2_h(0, 1)
+        mm2_h(1, 1)
         inter_h("S", 0, 1)
         inter_h("V", 1, 1)
-        mm2_p(0)
-        tanh(0)
-        mm2_p(1)
-        quant_w(("v", 1), 0)
-        mm2_s(0)
-        drain("S", ("v", 1), 1)
-        quant_h(1, 1)
         quant_h(0, 1)
-        drain("S", ("wh", 0), 1)
-        quant_w(("wh", 1), 1)
-        mm2_p(2)
-        mm2_s(1)
-        quant_w(("v", 1), 1)
+        tanh(0)
         add(0)
-        quant_w(("wh", 0), 1)
-        drain("S", ("wx", 0), 1)
-        drain("S", ("wx", 1), 1)
-        mm2_s(2)
+        mm2_h(2, 1)
         tanh(1)
-        quant_w(("wx", 0), 1)
-        sign(3)
+        mm2_h(3, 1)
         tanh(2)
-        quant_w(("wx", 1), 1)
-        add(1)
+        mm2_x(4)
+        mm2_x(5)
+        quant_h(1, 1)
         margin("G", 0)
-        inter("S", ("v", 0), 1)
+        add(1)
         add(2)
-        mm2_p(3)
-        mm2_s(3)
         margin("V", 1)
+        sign("S", 2)
+        tanh(3)
         expo(0)
         expo(1)
-        tanh(3)
         margin("V", 2)
-        quant_w(("v", 0), 1)
+        mm2_h(4, 0)
         target(0)
-        mm2_p(4)
-        mm2_p(5)
-        target(1)
+        mm2_h(5, 0)
         expo(2)
-        mm2_s(4)
         add(3)
-        mm2_s(5)
-        tanh(4)
-        tanh(5)
+        target(1)
         target(2)
-        margin("G", 3)
-        expo(3)
+        mm2_x(6)
+        mm2_h(4, 1)
+        mm2_h(5, 1)
+        tanh(4)
+        mm2_h(6, 0)
+        mm2_x(7)
+        tanh(5)
+        sign("S", 3)
+        mm2_x(8)
+        mm2_h(6, 1)
         add(4)
-        mm2_p(6)
-        mm2_s(6)
         add(5)
+        margin("G", 3)
         margin("V", 4)
-        tanh(6)
+        mm2_h(7, 0)
+        mm2_h(8, 0)
+        expo(3)
         margin("V", 5)
-        target(3)
-        mm2_s(7)
-        mm2_p(7)
-        add(6)
+        tanh(6)
         expo(4)
-        mm2_s(8)
-        target(4)
+        target(3)
         expo(5)
-        margin("V", 6)
-        target(5)
+        mm2_h(7, 1)
+        mm2_h(8, 1)
         tanh(7)
-        mm2_p(8)
-        tanh(8)
+        add(6)
+        target(4)
+        margin("V", 6)
         add(7)
-        add(8)
+        tanh(8)
+        target(5)
         expo(6)
-        target(6)
+        add(8)
         margin("V", 7)
-        margin("V", 8)
+        target(6)
         expo(7)
-        target(7)
+        margin("V", 8)
         expo(8)
+        target(7)
         target(8)

from contextlib import ExitStack

import concourse.mybir as mybir
from concourse.masks import make_identity

B, D, H, C = 1024, 1024, 1024, 512
FLOPS = 2 * B * D * H + 3 * 2 * B * D * C

F32 = mybir.dt.float32
BF16 = mybir.dt.bfloat16
U32 = mybir.dt.uint32
U8 = mybir.dt.uint8
FP8 = mybir.dt.float8_e4m3fn
FP8X4 = mybir.dt.float8_e4m3fn_x4
ALU = mybir.AluOpType
ACT = mybir.ActivationFunctionType

P = 128
LN2 = 0.6931471805599453


def tile_grownetnewtontargets_kernel(tc, x_bytes, x_scale, w1, g1, v1, wx, wh, u, out):
    nc = tc.nc
    with ExitStack() as ctx:
        keep = ctx.enter_context(tc.tile_pool(name="keep", bufs=1))
        stage = ctx.enter_context(tc.tile_pool(name="stage", bufs=3))
        psum = ctx.enter_context(tc.psum_pool(name="psum", bufs=8))
        ctx.enter_context(tc.manual_schedule())

        ident = keep.tile([P, P], F32, name="ident")
        make_identity(nc, ident[:])

        scale_cols = keep.tile([P, 8], F32, name="scale_cols")
        nc.sync.dma_start(out=scale_cols[:], in_=x_scale.rearrange("o (p m) -> p (o m)", m=8))
        ident_bf = keep.tile([P, P], BF16, name="ident_bf")
        nc.gpsimd.tensor_copy(out=ident_bf[:], in_=ident[:])
        warm = keep.tile([P, 1], F32, name="warm")
        nc.vector.memset(warm[:], 0.0)
        warm_out = keep.tile([P, 1], F32, name="warm_out")
        nc.scalar.activation(out=warm_out[:], in_=warm[:], func=ACT.Tanh)

        w1_raw = {}
        w1_view = w1.rearrange("(g p j) n -> g p j n", p=P, j=4)

        def load_w1(g, hg):
            t = keep.tile([P, 4, 512], BF16, name=f"w1_raw_{g}_{hg}")
            nc.sync.dma_start(out=t[:], in_=w1_view[g][:, :, hg * 512 : (hg + 1) * 512])
            w1_raw[g, hg] = t

        xb = {}
        x_view = x_bytes.rearrange("(p j) k -> p j k", j=8)

        def load_x(c):
            t = keep.tile([P, 2, D], U8, name=f"xb_{c}")
            nc.sync.dma_start(out=t[:], in_=x_view[:, 2 * c : 2 * c + 2, :])
            xb[c] = t

        w_raw = {}

        def load_w(name, ap):
            t = keep.tile([P, 2, 4, C], BF16, name=f"{name}_raw")
            nc.sync.dma_start(out=t[:], in_=ap.rearrange("(g p j) c -> p g j c", p=P, j=4))
            w_raw[name] = t

        load_w1(0, 0)
        load_x(0)
        load_w1(1, 0)
        load_x(1)
        load_x(2)
        load_w1(0, 1)
        load_x(3)
        load_w1(1, 1)
        load_w("wx", wx)
        load_w("v", v1)
        load_w("wh", wh)
        ub = keep.tile([P, 8, C], BF16, name="ub")
        nc.sync.dma_start(out=ub[:], in_=u.rearrange("(p j) c -> p j c", j=8))
        gain_bf = keep.tile([P, 2, 4], BF16, name="gain_bf")
        nc.gpsimd.dma_start(out=gain_bf[:], in_=g1.rearrange("(g p t) -> p g t", p=P, t=4))
        gain = keep.tile([P, 2, 4], F32, name="gain")
        nc.gpsimd.tensor_copy(out=gain[:], in_=gain_bf[:])

        scale = keep.tile([P, D], F32, name="scale")

        spread = {}

        def spread_scale(i):
            bank = psum.tile([P, 4, P], F32, name="bank")
            spread[i] = bank
            for m in range(4):
                column = scale_cols[:, 4 * i + m : 4 * i + m + 1]
                nc.tensor.transpose(bank[:, m, :], column.to_broadcast([P, P]), ident[:])

        def store_scale(engine, i):
            d = scale[:].rearrange("q (p m) -> q p m", m=8)[:, :, 4 * i : 4 * i + 4]
            s = spread[i][:].rearrange("q m p -> q p m")
            if engine == "S":
                nc.scalar.copy(out=d, in_=s)
            else:
                nc.vector.tensor_copy(out=d, in_=s)

        w_codes = {}
        w_scales = {}
        w_grouped = {}
        blends = {}

        def grouped(key, piece):
            if key[0] == "w1":
                if key not in w_grouped:
                    w_grouped[key] = stage.tile([P, 512, 4], BF16, name="w1g", bufs=3, align_bytes=64)
                return w_grouped[key]
            if (key, piece) not in w_grouped:
                w_grouped[key, piece] = stage.tile([P, 256, 4], BF16, name="wg", bufs=6, align_bytes=64)
            return w_grouped[key, piece]

        def inter(engine, key, piece):
            dst = grouped(key, piece)
            if key[0] == "w1":
                d = dst[:].rearrange("p (t m) j -> p m j t", t=4)[:, piece * 64 : (piece + 1) * 64]
                s = w1_raw[key[1], key[2]][:].rearrange("p j (m t) -> p m j t", t=4)[:, piece * 64 : (piece + 1) * 64]
            else:
                d = dst[:].rearrange("p (c i) t -> p c t i", i=4)
                s = w_raw[key[0]][:, key[1], :, piece * 256 : (piece + 1) * 256].rearrange("p t (c i) -> p c t i", i=4)
            if engine == "S":
                nc.scalar.copy(out=d, in_=s)
            else:
                nc.vector.tensor_copy(out=d, in_=s)

        def blend(key, piece):
            bank = psum.tile([P, 256, 4], BF16, name="bank")
            for i in range(2):
                c = 256 * piece + 128 * i
                nc.tensor.matmul(
                    bank[:, 128 * i : 128 * i + 128, :].rearrange("p (c i) t -> p c t i", i=4),
                    lhsT=ident_bf[:],
                    rhs=w_raw[key[0]][:, key[1], :, c : c + 128].rearrange("p t (c i) -> p c t i", i=4),
                    start=True, stop=True,
                )
            blends[key, piece] = bank

        def drain(engine, key, piece):
            d, s = grouped(key, piece)[:], blends[key, piece][:]
            if engine == "S":
                nc.scalar.copy(out=d, in_=s)
            else:
                nc.vector.tensor_copy(out=d, in_=s)

        def quant_w(key, piece=None):
            if key not in w_codes:
                tag = "_".join(str(k) for k in key)
                w_codes[key] = keep.tile([P, 512], U32, name=f"codes_{tag}", align_bytes=64)
                w_scales[key] = keep.tile([P, 512], U8, name=f"scales_{tag}", align_bytes=64)
            cols = slice(0, 512) if piece is None else slice(piece * 256, (piece + 1) * 256)
            nc.vector.quantize_mx(
                out=w_codes[key][:, cols].bitcast(FP8X4), scales=w_scales[key][:, cols],
                in_=grouped(key, piece)[:].rearrange("p c t -> p (c t)"),
            )

        xs = {}
        xt = {}
        xg = {}
        x_codes = [keep.tile([P, 2, 512], U32, name=f"x_codes_{i}", align_bytes=64) for i in range(2)]
        x_scales = [keep.tile([P, 2, 512], U8, name=f"x_scales_{i}", align_bytes=64) for i in range(2)]

        def widen(j):
            xs[j] = stage.tile([P, D], BF16, name="xs", bufs=4)
            nc.vector.tensor_tensor(out=xs[j][:], in0=xb[j // 2][:, j % 2, :].bitcast(FP8), in1=scale[:], op=ALU.mult)

        def turn(j):
            words = xs[j][:].bitcast(F32)
            xt[j] = psum.tile([P, 2, 2, P], F32, name="bank")
            for g in range(2):
                for e in range(2):
                    nc.tensor.transpose(xt[j][:, g, e, :], words[:, 256 * g + e : 256 * (g + 1) : 2], ident[:])

        def empty(engine, j):
            c = j // 2
            if j % 2 == 0:
                xg[c] = stage.tile([P, 2, 256, 4], BF16, name="xg", bufs=2, align_bytes=64)
            rows = slice((j % 2) * P, (j % 2 + 1) * P)
            d, s = xg[c][:].bitcast(F32)[:, :, rows, :], xt[j][:].rearrange("p g e r -> p g r e")
            if engine == "S":
                nc.scalar.copy(out=d, in_=s)
            else:
                nc.vector.tensor_copy(out=d, in_=s)

        def quant_x(c):
            for g in range(2):
                cols = slice((c % 2) * 256, (c % 2 + 1) * 256)
                nc.vector.quantize_mx(
                    out=x_codes[c // 2][:, g, cols].bitcast(FP8X4),
                    scales=x_scales[c // 2][:, g, cols],
                    in_=xg[c][:, g].rearrange("p r t -> p (r t)"),
                )

        def mx(acc, l_codes, l_scales, r_codes, r_scales, start, stop):
            nc.tensor.matmul_mx(
                out=acc, lhsT=l_codes.bitcast(FP8X4), lhsT_scale=l_scales, rhs=r_codes.bitcast(FP8X4), rhs_scale=r_scales,
                start=start, stop=stop,
            )

        r = [keep.tile([P, 4, B], F32, name=f"r_{i}") for i in range(2)]
        sums = [keep.tile([P, 2, 4], F32, name=f"sums_{i}") for i in range(2)]
        mean = [keep.tile([P, 4], F32, name=f"mean_{i}") for i in range(2)]
        shift = [keep.tile([P, 4], F32, name=f"shift_{i}") for i in range(2)]
        hc = [keep.tile([P, 4, B], BF16, name=f"hc_{i}") for i in range(2)]
        h_grouped = {}
        h_codes = [keep.tile([P, B], U32, name=f"h_codes_{i}", align_bytes=64) for i in range(2)]
        h_scales = [keep.tile([P, B], U8, name=f"h_scales_{i}", align_bytes=64) for i in range(2)]
        acc1 = {}

        def mm1(hg, half, t):
            acc = psum.tile([P, 512], F32, name="bank")
            for g in range(2):
                cols = slice(t * P, (t + 1) * P)
                key = ("w1", g, hg)
                mx(acc[:], w_codes[key][:, cols], w_scales[key][:, cols], x_codes[half][:, g, :], x_scales[half][:, g, :], g == 0, g == 1)
            acc1[hg, half, t] = acc

        def relu(hg, half, t):
            nc.scalar.activation(
                out=r[hg][:, t, half * 512 : (half + 1) * 512], in_=acc1[hg, half, t][:], func=ACT.Relu,
                accum_out=sums[hg][:, half, t : t + 1],
            )

        totals = {}

        def total(hg):
            totals[hg] = stage.tile([P, 4], F32, name="total")
            nc.vector.tensor_tensor(out=totals[hg][:], in0=sums[hg][:, 0, :], in1=sums[hg][:, 1, :], op=ALU.add)

        def average(hg):
            nc.vector.tensor_scalar(out=mean[hg][:], in0=totals[hg][:], scalar1=1.0 / B, scalar2=None, op0=ALU.mult)

        def offset(hg):
            nc.vector.scalar_tensor_tensor(out=shift[hg][:], in0=mean[hg][:], scalar=-1.0, in1=gain[:, hg, :], op0=ALU.mult, op1=ALU.mult)

        def center(engine, hg, half, t):
            cols = slice(half * 512, (half + 1) * 512)
            d, s = hc[hg][:, t, cols], r[hg][:, t, cols]
            if engine == "S":
                nc.scalar.activation(out=d, in_=s, func=ACT.Identity, scale=gain[:, hg, t : t + 1], bias=shift[hg][:, t : t + 1])
            else:
                nc.vector.tensor_scalar(
                    out=d, in0=s, scalar1=mean[hg][:, t : t + 1], scalar2=gain[:, hg, t : t + 1],
                    op0=ALU.subtract, op1=ALU.mult,
                )

        def inter_h(engine, hg, half):
            t = stage.tile([P, 512, 4], BF16, name="hgrp", bufs=3, align_bytes=64)
            h_grouped[hg, half] = t
            d = t[:].rearrange("p (c i) t -> p c t i", i=4)
            s = hc[hg][:, :, half * 512 : (half + 1) * 512].rearrange("p t (c i) -> p c t i", i=4)
            if engine == "S":
                nc.scalar.copy(out=d, in_=s)
            else:
                nc.vector.tensor_copy(out=d, in_=s)

        def quant_h(hg, half):
            cols = slice(half * 512, (half + 1) * 512)
            nc.vector.quantize_mx(
                out=h_codes[hg][:, cols].bitcast(FP8X4), scales=h_scales[hg][:, cols],
                in_=h_grouped[hg, half][:].rearrange("p c t -> p (c t)"),
            )

        y_half = keep.tile([P, 8, C], BF16, name="y_half")
        units = [(k, 0, C) for k in range(7)] + [(7, 0, C // 2), (7, C // 2, C)]
        pb = {}
        sb = {}

        y_size = {}

        def sign(engine, jp):
            js = slice(2 * jp, 2 * jp + 2)
            y_size[2 * jp] = y_size[2 * jp + 1] = 1.0 if engine == "S" else 0.5
            if engine == "S":
                nc.scalar.activation(out=y_half[:, js, :], in_=ub[:, js, :], func=ACT.Sign, scale=2.0**20, bias=2.0**-120)
                return
            nc.vector.tensor_scalar(
                out=y_half[:, js, :], in0=ub[:, js, :], scalar1=0.0, scalar2=0.5, op0=ALU.is_ge, op1=ALU.subtract
            )

        def x_cols(g, j):
            return x_codes[j // 4][:, g, (j % 4) * P : (j % 4 + 1) * P], x_scales[j // 4][:, g, (j % 4) * P : (j % 4 + 1) * P]

        def h_cols(hg, j):
            return h_codes[hg][:, j * P : (j + 1) * P], h_scales[hg][:, j * P : (j + 1) * P]

        def mm2_x(k):
            j, lo, hi = units[k]
            pb[k] = psum.tile([P, hi - lo], F32, name="bank")
            for g in range(2):
                mx(pb[k][:], *x_cols(g, j), w_codes["wx", g][:, lo:hi], w_scales["wx", g][:, lo:hi], g == 0, False)

        def mm2_h(k, hg):
            j, lo, hi = units[k]
            if hg == 0:
                sb[k] = psum.tile([P, hi - lo], F32, name="bank")
            mx(pb[k][:], *h_cols(hg, j), w_codes["wh", hg][:, lo:hi], w_scales["wh", hg][:, lo:hi], False, hg == 1)
            mx(sb[k][:], *h_cols(hg, j), w_codes["v", hg][:, lo:hi], w_scales["v", hg][:, lo:hi], hg == 0, hg == 1)

        work = {}

        def y_of(k):
            j, lo, hi = units[k]
            return y_half[:, j, lo:hi]

        def tanh(k):
            j, lo, hi = units[k]
            work[k] = stage.tile([P, hi - lo], F32, name="work", bufs=6)
            nc.scalar.activation(out=work[k][:], in_=pb[k][:], func=ACT.Tanh)

        def add(k):
            nc.vector.tensor_tensor(out=work[k][:], in0=sb[k][:], in1=work[k][:], op=ALU.add)

        def margin(engine, k):
            (nc.gpsimd if engine == "G" else nc.vector).tensor_tensor(out=work[k][:], in0=work[k][:], in1=y_of(k), op=ALU.mult)

        def expo(k):
            size = y_size[units[k][0]]
            nc.scalar.activation(
                out=work[k][:], in_=work[k][:], func=ACT.Exp, scale=-0.8 / size, bias=0.0 if size == 1.0 else LN2
            )

        def target(k):
            j, lo, hi = units[k]
            nc.vector.scalar_tensor_tensor(
                out=work[k][:], in0=work[k][:], scalar=1.0 / y_size[j], in1=y_of(k), op0=ALU.add, op1=ALU.mult
            )
            nc.sync.dma_start(out=out.rearrange("(p j) c -> p j c", j=8)[:, j, lo:hi], in_=work[k][:])

        inter("S", ("w1", 0, 0), 0)
        inter("V", ("w1", 0, 0), 1)
        spread_scale(0)
        spread_scale(1)
        store_scale("V", 0)
        store_scale("S", 1)
        inter("S", ("w1", 1, 0), 0)
        inter("S", ("w1", 1, 0), 1)
        quant_w(("w1", 0, 0))
        inter("S", ("w1", 0, 1), 0)
        widen(0)
        turn(0)
        empty("S", 0)
        widen(1)
        inter("S", ("w1", 0, 1), 1)
        widen(2)
        inter("S", ("w1", 1, 1), 0)
        turn(1)
        turn(2)
        empty("S", 1)
        widen(3)
        widen(4)
        turn(3)
        turn(4)
        empty("S", 2)
        blend(("wx", 0), 1)
        widen(5)
        empty("S", 3)
        turn(5)
        widen(6)
        widen(7)
        quant_x(0)
        inter("S", ("wx", 0), 0)
        quant_w(("w1", 1, 0))
        quant_x(1)
        inter("V", ("wx", 1), 0)
        inter("S", ("w1", 1, 1), 1)
        empty("S", 4)
        turn(6)
        empty("S", 5)
        quant_w(("w1", 0, 1))
        quant_w(("w1", 1, 1))
        turn(7)
        inter("V", ("wx", 1), 1)
        blend(("v", 1), 0)
        mm1(0, 0, 0)
        mm1(0, 0, 1)
        mm1(0, 0, 2)
        empty("S", 6)
        empty("S", 7)
        drain("S", ("wx", 0), 1)
        mm1(0, 0, 3)
        quant_x(2)
        mm1(1, 0, 0)
        drain("S", ("v", 1), 0)
        relu(0, 0, 0)
        quant_x(3)
        quant_w(("wx", 1), 0)
        relu(0, 0, 1)
        mm1(0, 1, 0)
        quant_w(("wx", 0), 0)
        quant_w(("wx", 1), 1)
        mm1(0, 1, 1)
        quant_w(("v", 1), 0)
        mm1(0, 1, 2)
        sign("V", 0)
        mm1(0, 1, 3)
        relu(0, 0, 2)
        inter("V", ("wh", 1), 0)
        inter("V", ("v", 0), 0)
        mm1(1, 0, 1)
        mm1(1, 0, 2)
        relu(0, 0, 3)
        quant_w(("wx", 0), 1)
        relu(0, 1, 0)
        relu(0, 1, 1)
        relu(0, 1, 2)
        relu(0, 1, 3)
        inter("V", ("v", 0), 1)
        relu(1, 0, 0)
        quant_w(("v", 0), 0)
        mm1(1, 1, 0)
        inter("V", ("wh", 0), 0)
        mm1(1, 1, 1)
        total(0)
        quant_w(("wh", 1), 0)
        relu(1, 0, 1)
        relu(1, 0, 2)
        relu(1, 1, 0)
        mm1(1, 1, 2)
        quant_w(("wh", 0), 0)
        average(0)
        inter("V", ("wh", 0), 1)
        center("V", 0, 0, 0)
        mm1(1, 1, 3)
        center("V", 0, 0, 1)
        mm1(1, 0, 3)
        blend(("v", 1), 1)
        relu(1, 1, 1)
        mm2_x(0)
        center("V", 0, 0, 2)
        mm2_x(1)
        center("V", 0, 0, 3)
        offset(0)
        quant_w(("wh", 0), 1)
        relu(1, 1, 2)
        relu(1, 1, 3)
        relu(1, 0, 3)
        inter("S", ("wh", 1), 1)
        inter_h("V", 0, 0)
        quant_w(("v", 0), 1)
        total(1)
        center("S", 0, 1, 0)
        mm2_x(2)
        quant_h(0, 0)
        average(1)
        center("V", 0, 1, 1)
        center("V", 0, 1, 2)
        drain("S", ("v", 1), 1)
        offset(1)
        center("V", 1, 0, 0)
        mm2_h(0, 0)
        center("V", 1, 0, 1)
        center("V", 1, 0, 2)
        quant_w(("wh", 1), 1)
        center("S", 1, 0, 3)
        center("S", 1, 1, 0)
        mm2_h(1, 0)
        mm2_x(3)
        center("V", 1, 1, 1)
        inter_h("V", 1, 0)
        quant_w(("v", 1), 1)
        center("S", 0, 1, 3)
        mm2_h(2, 0)
        quant_h(1, 0)
        mm2_h(3, 0)
        center("V", 1, 1, 2)
        center("S", 1, 1, 3)
        sign("V", 1)
        mm2_h(0, 1)
        mm2_h(1, 1)
        inter_h("S", 0, 1)
        inter_h("V", 1, 1)
        quant_h(0, 1)
        tanh(0)
        add(0)
        mm2_h(2, 1)
        tanh(1)
        mm2_h(3, 1)
        tanh(2)
        mm2_x(4)
        mm2_x(5)
        quant_h(1, 1)
        margin("G", 0)
        add(1)
        add(2)
        margin("V", 1)
        sign("S", 2)
        tanh(3)
        expo(0)
        expo(1)
        margin("V", 2)
        mm2_h(4, 0)
        target(0)
        mm2_h(5, 0)
        expo(2)
        add(3)
        target(1)
        target(2)
        mm2_x(6)
        mm2_h(4, 1)
        mm2_h(5, 1)
        tanh(4)
        mm2_h(6, 0)
        mm2_x(7)
        tanh(5)
        sign("S", 3)
        mm2_x(8)
        mm2_h(6, 1)
        add(4)
        add(5)
        margin("G", 3)
        margin("V", 4)
        mm2_h(7, 0)
        mm2_h(8, 0)
        expo(3)
        margin("V", 5)
        tanh(6)
        expo(4)
        target(3)
        expo(5)
        mm2_h(7, 1)
        mm2_h(8, 1)
        tanh(7)
        add(6)
        target(4)
        margin("V", 6)
        add(7)
        tanh(8)
        target(5)
        expo(6)
        add(8)
        margin("V", 7)
        target(6)
        expo(7)
        margin("V", 8)
        expo(8)
        target(7)
        target(8)
